import numpy as np
import ml_dtypes


def mxq(x, axis, fmt="e4m3"):
    dtype, down = {"e4m3": (ml_dtypes.float8_e4m3fn, 7), "e5m2": (ml_dtypes.float8_e5m2, 14)}[fmt]
    v = np.moveaxis(np.asarray(x, np.float32).astype(ml_dtypes.bfloat16).astype(np.float64), axis, -1)
    blocks = v.reshape(v.shape[:-1] + (-1, 32))
    amax = np.abs(blocks).max(-1, keepdims=True)
    byte = np.maximum(np.where(amax > 0, np.frexp(amax)[1] - 1 + 127, 0) - down, 1)
    scale = np.exp2(byte - 127.0)
    codes = (blocks / scale).astype(np.float32).astype(dtype).astype(np.float64)
    return np.moveaxis((codes * scale).reshape(v.shape), -1, axis)


WIDE = False


def mx_kscale(k):
    if not WIDE:
        return np.ones(k)
    levels = np.array([10, -10, 5, -5, 0])
    if k % 512:
        return np.exp2(np.random.permutation(np.resize(levels, k // 32))).repeat(32)
    a = np.empty((k // 512, 16))
    for p in range(k // 512):
        a[p, :8] = np.random.permutation(np.resize(levels, 8))
        for g in range(8):
            far = levels[np.abs(levels - a[p, g]) >= 10]
            a[p, g + 8] = far[np.random.randint(len(far))]
    return np.exp2(a.ravel()).repeat(32)


def f64(x):
    return np.asarray(x).astype(np.float64)


def striped(idx):
    return np.tile(idx.reshape(-1, 16).T, (8, 1)).astype(np.uint16)


def unstriped(offs):
    return offs[:16].T.reshape(-1).astype(np.int64)


E2M1 = np.array([0.0, 0.5, 1.0, 1.5, 2.0, 3.0, 4.0, 6.0, -0.0, -0.5, -1.0, -1.5, -2.0, -3.0, -4.0, -6.0])


def pack_weight(w, fmt):
    k, n = w.shape
    w = f64(np.asarray(w, np.float32).astype(ml_dtypes.bfloat16)).reshape(k // 32, 32, n)
    amax = np.abs(w).max(1)
    if fmt == "e4m3":
        byte = np.frexp(amax)[1] - 1 + 127 - 7
    else:
        mant, ex = np.frexp(amax / 6.0)
        byte = np.where(mant > 0.5, ex, ex - 1) + 127
    byte = np.clip(np.where(amax > 0, byte, 1), 1, 254)
    scaled = (w * np.exp2(127.0 - byte)[:, None, :]).reshape(k, n).astype(np.float32)
    by_word = np.ascontiguousarray(scaled.reshape(k // 512, 128, 4, n).transpose(0, 1, 3, 2))
    if fmt == "e4m3":
        words = by_word.astype(ml_dtypes.float8_e4m3fn).view(np.uint8)
    else:
        c = by_word.astype(ml_dtypes.float4_e2m1fn).view(np.uint8) & 0xF
        words = (c[..., 0::2] | (c[..., 1::2] << 4)).reshape(k // 512, 128, 2 * n)
    return np.ascontiguousarray(words), np.ascontiguousarray(byte.astype(np.uint8).reshape(k // 512, 16, n))


def unpack_weight(words, scales, fmt):
    g, _, n = scales.shape
    words = np.ascontiguousarray(words).reshape(g, 128, n, -1)
    if fmt == "e4m3":
        vals = words.view(ml_dtypes.float8_e4m3fn).astype(np.float64)
    else:
        nib = np.empty((g, 128, n, 4), np.uint8)
        nib[..., 0::2] = words & 0xF
        nib[..., 1::2] = words >> 4
        vals = E2M1[nib]
    vals = vals * np.repeat(np.exp2(scales.astype(np.float64) - 127.0), 8, axis=1)[..., None]
    return vals.transpose(0, 1, 3, 2).reshape(g * 512, n)


def gelu(v):
    return 0.5 * v * (1.0 + np.tanh(np.sqrt(2.0 / np.pi) * (v + 0.044715 * v**3)))


K, K1, T, S, H, S2, T3 = 1536, 1024, 2048, 512, 1024, 512, 2048

def setup_inputs():
    n = np.random.standard_normal
    s = mx_kscale(K)[:, None]
    u = mx_kscale(H)[:, None]
    tab_words, tab_scales = pack_weight(n((K, T)) * s, "e4m3")
    w4_words, w4_scales = pack_weight(0.48 * n((K1, H)) / np.sqrt(K) / s[:K1], "e2m1")
    w1 = (0.48 * n((K - K1, H)) / np.sqrt(K) / s[K1:]).astype(np.float32)
    b1 = np.random.uniform(-0.5, 0.5, H).astype(np.float32)
    gp = (np.exp(0.3 * n(H)) * u[:, 0]).astype(np.float32)
    gv = (np.exp(0.3 * n(H)) * u[:, 0]).astype(np.float32)
    tab2_words, tab2_scales = pack_weight(n((H, T3)) / np.sqrt(H) / u, "e4m3")
    tab3_words, tab3_scales = pack_weight(n((H, T3)) / np.sqrt(H) / u, "e4m3")
    d = (1.6 * np.exp(0.4 * n(S2))).astype(np.float32)
    return {"tab_words": tab_words, "tab_scales": tab_scales,
            "offs": striped(np.random.permutation(T)[:S]),
            "w4_words": w4_words, "w4_scales": w4_scales, "w1": w1, "b1": b1,
            "gp": gp, "gv": gv,
            "tab2_words": tab2_words, "tab2_scales": tab2_scales,
            "offs2": striped(np.random.permutation(T3)[:S2]),
            "tab3_words": tab3_words, "tab3_scales": tab3_scales,
            "offs3": striped(np.random.permutation(T3)[:S2]), "d": d}

def reference(tab_words, tab_scales, offs, w4_words, w4_scales, w1, b1, gp, gv,
              tab2_words, tab2_scales, offs2, tab3_words, tab3_scales, offs3, d):
    v = unpack_weight(tab_words, tab_scales, "e4m3")[:, unstriped(offs)]
    v2 = unpack_weight(tab2_words, tab2_scales, "e4m3")[:, unstriped(offs2)]
    v3 = unpack_weight(tab3_words, tab3_scales, "e4m3")[:, unstriped(offs3)]
    w4 = unpack_weight(w4_words, w4_scales, "e2m1")
    w1q = mxq(f64(w1), 0, "e4m3")
    a = (w4.T @ v[:K1] + w1q.T @ v[K1:]) + f64(b1)[:, None]
    h = mxq(np.tanh(a) * f64(gp)[:, None], 0, "e4m3")
    x = mxq(np.cos(a) * f64(gv)[:, None], 0, "e4m3")
    e2 = v2.T @ h
    e3 = v3.T @ x
    return f64(d)[:, None] * e2 + e3

@@ -1,0 +1,304 @@
+from contextlib import ExitStack
+
+import concourse.mybir as mybir
+
+K, K1, T, S, H, S2 = 1536, 1024, 2048, 512, 1024, 512
+FLOPS = 2 * K * H * S + 2 * 2 * H * S2 * S
+
+F32 = mybir.dt.float32
+BF16 = mybir.dt.bfloat16
+I32 = mybir.dt.int32
+U32 = mybir.dt.uint32
+U16 = mybir.dt.uint16
+U8 = mybir.dt.uint8
+FP8X4 = mybir.dt.float8_e4m3fn_x4
+FP4X4 = mybir.dt.float4_e2m1fn_x4
+ACT = mybir.ActivationFunctionType
+ALU = mybir.AluOpType
+
+P = 128
+PACK = 4
+KP = P * PACK
+V_PASSES = K // KP
+W4_PASSES = K1 // KP
+R_PASSES = H // KP
+JW = 256
+J_CHUNKS = S // JW
+M_TILES = S2 // P
+LIST_COLS = 16
+QUADS = 4
+LINE = 4
+BANK = 512
+LAST_CHUNKS = ((0, 256), (256, 128), (384, 128))
+
+
+def tile_list_foursome_invitation_scores_kernel(
+    tc, tab_words, tab_scales, offs, w4_words, w4_scales, w1, b1, gp, gv,
+    tab2_words, tab2_scales, offs2, tab3_words, tab3_scales, offs3, d, out,
+):
+    nc = tc.nc
+    with ExitStack() as ctx:
+        lists = ctx.enter_context(tc.tile_pool(name="lists", bufs=1))
+        keep = ctx.enter_context(tc.tile_pool(name="keep", bufs=1))
+        big = ctx.enter_context(tc.tile_pool(name="big", bufs=1))
+        work = ctx.enter_context(tc.tile_pool(name="work", bufs=2))
+        psum_a = ctx.enter_context(tc.psum_pool(name="psum_a", bufs=4))
+        psum_e = ctx.enter_context(tc.psum_pool(name="psum_e", bufs=4))
+
+        def held(shape, dtype, name):
+            return keep.tile(shape, dtype, name=name, align_bytes=64)
+
+        idx = lists.tile([P, S // LIST_COLS], U16, name="idx")
+        idx2 = lists.tile([P, S2 // LIST_COLS], U16, name="idx2")
+        idx3 = lists.tile([P, S2 // LIST_COLS], U16, name="idx3")
+        nc.sync.dma_start(idx[:], offs)
+        nc.sync.dma_start(idx2[:], offs2)
+        nc.sync.dma_start(idx3[:], offs3)
+
+        def load_rows(name, rows, width, src):
+            tile = big.tile([P, width], U8, name=name, align_bytes=64)
+            nc.scalar.dma_start(tile[P - rows : P, :].bitcast(I32), src.bitcast(I32))
+            nc.vector.memset(tile[0 : P - rows, :].bitcast(I32), 0)
+            return tile
+
+        w4s_rows = load_rows("buf_a", 16 * W4_PASSES, H, w4_scales.rearrange("a q c -> q a c"))
+        vs_rows = load_rows("buf_b", 16 * V_PASSES, T, tab_scales.rearrange("a q t -> q a t"))
+        v2s_rows = load_rows("v2s_rows", 16 * R_PASSES, T, tab2_scales.rearrange("a q t -> q a t"))
+        v3s_rows = load_rows("v3s_rows", 16 * R_PASSES, T, tab3_scales.rearrange("a q t -> q a t"))
+
+        w4_planes = held([P, W4_PASSES * H], U8, "w4_planes")
+        v_planes = held([P, V_PASSES * S], U8, "v_planes")
+        c_planes = held([P, R_PASSES * 2 * S2], U8, "c_planes")
+        for planes in (w4_planes, v_planes, c_planes):
+            nc.vector.memset(planes[:].bitcast(I32), 0)
+
+        def place_rows(queue, planes, rows, count):
+            per_quad = count // QUADS
+            for q in range(QUADS):
+                r0 = P - count + per_quad * q
+                queue.dma_start(planes[32 * q : 32 * q + 4, :].bitcast(I32), rows[r0 : r0 + per_quad, :].bitcast(I32))
+
+        b1_sb = held([P, R_PASSES, PACK], F32, "b1_sb")
+        gp_sb = held([P, R_PASSES, PACK], F32, "gp_sb")
+        gv_sb = held([P, R_PASSES, PACK], F32, "gv_sb")
+        d_sb = held([P, M_TILES], F32, "d_sb")
+        for tile, vec in ((b1_sb, b1), (gp_sb, gp), (gv_sb, gv)):
+            nc.gpsimd.dma_start(tile[:], vec.rearrange("(b p t) -> p b t", p=P, t=PACK))
+        with nc.allow_non_contiguous_dma(reason="one value of d for each output row"):
+            nc.gpsimd.dma_start(d_sb[:], d.rearrange("(u p) -> p u", p=P))
+
+        w1_rows = w1.rearrange("(p j) c -> p j c", j=PACK)
+
+        def load_w1(b):
+            tile = big.tile([P, PACK, KP], F32, name="buf_w", align_bytes=64)
+            nc.sync.dma_start(tile[:], w1_rows[:, :, b * KP : (b + 1) * KP])
+            return tile
+
+        def load_words(words, a, buf):
+            tile = big.tile([P, T], U32, name=buf, align_bytes=64)
+            nc.sync.dma_start(tile[:].bitcast(I32), words[a].rearrange("p t i -> p (t i)").bitcast(I32))
+            return tile
+
+        w1_raw = [load_w1(0)]
+        w4_raw = held([P, W4_PASSES, 2 * H], U8, "w4_raw")
+        nc.sync.dma_start(w4_raw[:].bitcast(I32), w4_words.rearrange("a p n -> p a n").bitcast(I32))
+        v_tab = [load_words(tab_words, 0, "buf_0")]
+
+        w4s_dealt = held([P, H], U8, "w4s_dealt")
+        nc.vector.tensor_copy(
+            out=w4s_dealt[:].rearrange("p (b t c i) -> p b c t i", b=R_PASSES, t=PACK, i=16),
+            in_=w4s_rows[:].rearrange("p (b c i t) -> p b c t i", b=R_PASSES, t=PACK, i=16),
+        )
+        place_rows(nc.scalar, w4_planes, w4s_dealt, 16 * W4_PASSES)
+        v_tab.append(load_words(tab_words, 1, "buf_a"))
+        vs_picked = held([P, S], U8, "vs_picked")
+        nc.vector.tensor_copy(vs_picked[:], vs_rows[:].indirect(idx[:]))
+        place_rows(nc.scalar, v_planes, vs_picked, 16 * V_PASSES)
+        v_tab.append(load_words(tab_words, 2, "buf_b"))
+
+        w4_dealt = [held([P, W4_PASSES, 2 * KP], U8, f"w4_dealt{b}") for b in range(R_PASSES)]
+        w1_bf = [held([P, PACK, P, PACK], BF16, f"w1_bf{b}") for b in range(R_PASSES)]
+        w1_codes = [held([P, KP], U32, f"w1_codes{b}") for b in range(R_PASSES)]
+        w1_scales = [held([P, KP], U8, f"w1_scales{b}") for b in range(R_PASSES)]
+
+        def deal_w1(b, copy):
+            copy(
+                out=w1_bf[b][:].rearrange("p t m j -> p m t j"),
+                in_=w1_raw[b][:].rearrange("p j (m t) -> p m t j", t=PACK),
+            )
+
+        def quantize_w1(b):
+            nc.vector.quantize_mx(
+                out=w1_codes[b][:].bitcast(FP8X4), scales=w1_scales[b][:],
+                in_=w1_bf[b][:].rearrange("p t m j -> p (t m j)"),
+            )
+
+        def deal_w4(b):
+            src = w4_raw[:].bitcast(U16)[:, :, b * KP : (b + 1) * KP]
+            nc.scalar.copy(
+                out=w4_dealt[b][:].bitcast(U16).rearrange("p a (t c i) -> p a c t i", t=PACK, i=8),
+                in_=src.rearrange("p a (c i t) -> p a c t i", t=PACK, i=8),
+            )
+
+        deal_w1(0, nc.scalar.copy)
+        w1_raw.append(load_w1(1))
+        deal_w4(0)
+        quantize_w1(0)
+
+        cs_picked = held([P, 2 * S2], U8, "cs_picked")
+        nc.vector.tensor_copy(cs_picked[:, 0:S2], v2s_rows[:].indirect(idx2[:]))
+        nc.vector.tensor_copy(cs_picked[:, S2 : 2 * S2], v3s_rows[:].indirect(idx3[:]))
+        place_rows(nc.gpsimd, c_planes, cs_picked, 16 * R_PASSES)
+        deal_w4(1)
+
+        half_b1 = held([P, R_PASSES, PACK], F32, "half_b1")
+        gv_m2 = held([P, R_PASSES, PACK], F32, "gv_m2")
+        nc.vector.tensor_scalar(out=half_b1[:], in0=b1_sb[:], scalar1=0.5, scalar2=None, op0=ALU.mult)
+        nc.vector.tensor_scalar(out=gv_m2[:], in0=gv_sb[:], scalar1=-2.0, scalar2=None, op0=ALU.mult)
+
+        cols = JW // LIST_COLS
+        v_picked = {}
+        for a in range(V_PASSES):
+            for jc in range(J_CHUNKS):
+                v_picked[a, jc] = held([P, JW], U32, f"v_picked{a}_{jc}")
+                nc.vector.tensor_copy(v_picked[a, jc][:], v_tab[a][:].indirect(idx[:, jc * cols : (jc + 1) * cols]))
+
+        v2_tab, v3_tab = [load_words(tab2_words, 0, "buf_0")], [load_words(tab3_words, 0, "buf_a")]
+        v2_tab.append(load_words(tab2_words, 1, "buf_b"))
+
+        def new_banks(pool, tag, width):
+            per_bank = BANK // width
+            banks = [pool.tile([P, per_bank, width], F32, name=tag) for slot in range(PACK // per_bank)]
+            return banks, per_bank
+
+        def stage1_pass(group, b, j0, width, a):
+            banks, per_bank = group
+            jc, off = divmod(j0, JW)
+            for t in range(PACK):
+                if a < W4_PASSES:
+                    lhsT = w4_dealt[b][:, a, 2 * P * t : 2 * P * (t + 1)].bitcast(FP4X4)
+                    c0 = a * H + b * KP + P * t
+                    lhsT_scale = w4_planes[:, c0 : c0 + P]
+                else:
+                    lhsT = w1_codes[b][:, P * t : P * (t + 1)].bitcast(FP8X4)
+                    lhsT_scale = w1_scales[b][:, P * t : P * (t + 1)]
+                nc.tensor.matmul_mx(
+                    out=banks[t // per_bank][:, t % per_bank, :], lhsT=lhsT, lhsT_scale=lhsT_scale,
+                    rhs=v_picked[a, jc][:, off : off + width].bitcast(FP8X4),
+                    rhs_scale=v_planes[:, a * S + j0 : a * S + j0 + width],
+                    start=(a == 0 and t % per_bank == 0), stop=(a == V_PASSES - 1 and t % per_bank == per_bank - 1),
+                )
+
+        rounded, codes, scales = {}, {}, {}
+
+        def quantize(kind, b, j0, width):
+            codes[kind, b, j0] = held([P, width], U32, f"{kind}_codes{b}_{j0}")
+            scales[kind, b, j0] = held([P, width], U8, f"{kind}_scales{b}_{j0}")
+            nc.vector.quantize_mx(
+                out=codes[kind, b, j0][:].bitcast(FP8X4), scales=scales[kind, b, j0][:],
+                in_=rounded[kind, b, j0][:].rearrange("p j t -> p (j t)"),
+            )
+
+        def make_h(group, b, j0, width):
+            banks, per_bank = group
+            th = work.tile([P, PACK, width], F32, name="th")
+            for t in range(PACK):
+                nc.scalar.activation(out=th[:, t, :], in_=banks[t // per_bank][:, t % per_bank, :], func=ACT.Tanh, bias=b1_sb[:, b, t : t + 1])
+            rounded["h", b, j0] = work.tile([P, width, PACK], BF16, name="h_bf", align_bytes=64)
+            nc.vector.tensor_tensor(
+                out=rounded["h", b, j0][:].rearrange("p (c i) t -> p c t i", i=LINE),
+                in0=th[:].rearrange("p t (c i) -> p c t i", i=LINE),
+                in1=gp_sb[:, b, :].unsqueeze(1).unsqueeze(3).to_broadcast([P, width // LINE, PACK, LINE]),
+                op=ALU.mult,
+            )
+
+        def make_x(group, b, j0, width):
+            banks, per_bank = group
+            sn = work.tile([P, PACK, width], F32, name="sn")
+            sq = work.tile([P, width, PACK], F32, name="sq")
+            for t in range(PACK):
+                nc.scalar.activation(out=sn[:, t, :], in_=banks[t // per_bank][:, t % per_bank, :], func=ACT.Sin, bias=half_b1[:, b, t : t + 1], scale=0.5)
+            nc.scalar.activation(
+                out=sq[:].rearrange("p (c i) t -> p c t i", i=LINE),
+                in_=sn[:].rearrange("p t (c i) -> p c t i", i=LINE), func=ACT.Square,
+            )
+            rounded["x", b, j0] = work.tile([P, width, PACK], BF16, name="x_bf", align_bytes=64)
+            nc.vector.scalar_tensor_tensor(
+                out=rounded["x", b, j0][:], in0=sq[:], scalar=-0.5,
+                in1=gv_m2[:, b, :].unsqueeze(1).to_broadcast([P, width, PACK]), op0=ALU.add, op1=ALU.mult,
+            )
+
+        c_picked = {}
+
+        def gather_candidates(n, b):
+            tabs, lst = ((v2_tab, idx2), (v3_tab, idx3))[n]
+            c_picked[n, b] = held([P, S2], U32, f"c_picked{n}_{b}")
+            nc.vector.tensor_copy(c_picked[n, b][:], tabs[b][:].indirect(lst[:]))
+
+        def stage2_pass(group, n, kind, b, j0, width):
+            banks, per_bank = group
+            first = j0 if b == R_PASSES - 1 else j0 // JW * JW
+            off = j0 - first
+            for u in range(M_TILES):
+                c0 = (2 * b + n) * S2 + P * u
+                nc.tensor.matmul_mx(
+                    out=banks[u // per_bank][:, u % per_bank, :],
+                    lhsT=c_picked[n, b][:, P * u : P * (u + 1)].bitcast(FP8X4), lhsT_scale=c_planes[:, c0 : c0 + P],
+                    rhs=codes[kind, b, first][:, off : off + width].bitcast(FP8X4),
+                    rhs_scale=scales[kind, b, first][:, off : off + width],
+                    start=(b == 0 and u % per_bank == 0), stop=(b == R_PASSES - 1 and u % per_bank == per_bank - 1),
+                )
+
+        out_rows = out.rearrange("(u p) j -> p u j", p=P)
+
+        def finish(j0, width):
+            e2 = new_banks(psum_e, "e_bank", width)
+            e3 = new_banks(psum_e, "e_bank", width)
+            per_bank = e2[1]
+            for b in range(R_PASSES):
+                stage2_pass(e2, 0, "h", b, j0, width)
+                stage2_pass(e3, 1, "x", b, j0, width)
+            de2 = work.tile([P, M_TILES, width], F32, name="de2")
+            res = work.tile([P, M_TILES, width], F32, name="res")
+            for u in range(M_TILES):
+                nc.scalar.activation(out=de2[:, u, :], in_=e2[0][u // per_bank][:, u % per_bank, :], func=ACT.Copy, scale=d_sb[:, u : u + 1])
+            for g, bank in enumerate(e3[0]):
+                tiles = slice(per_bank * g, per_bank * (g + 1))
+                nc.vector.tensor_tensor(out=res[:, tiles, :], in0=bank[:], in1=de2[:, tiles, :], op=ALU.add)
+                nc.sync.dma_start(out_rows[:, tiles, j0 : j0 + width], res[:, tiles, :])
+
+        first = [new_banks(psum_a, "a_bank", JW) for chunk in range(J_CHUNKS)]
+        for a in range(V_PASSES):
+            for jc in range(J_CHUNKS):
+                stage1_pass(first[jc], 0, jc * JW, JW, a)
+        make_h(first[0], 0, 0, JW)
+        deal_w1(1, nc.vector.tensor_copy)
+        v3_tab.append(load_words(tab3_words, 1, "buf_w"))
+        make_x(first[0], 0, 0, JW)
+        quantize_w1(1)
+        quantize("h", 0, 0, JW)
+        make_h(first[1], 0, JW, JW)
+        quantize("x", 0, 0, JW)
+        gather_candidates(0, 0)
+        make_x(first[1], 0, JW, JW)
+        quantize("h", 0, JW, JW)
+        gather_candidates(1, 0)
+        quantize("x", 0, JW, JW)
+        before = None
+        for j0, width in LAST_CHUNKS:
+            group = new_banks(psum_a, "a_bank", width)
+            for a in range(V_PASSES):
+                stage1_pass(group, 1, j0, width, a)
+            make_h(group, 1, j0, width)
+            if before is None:
+                gather_candidates(0, 1)
+            else:
+                quantize("x", 1, *before)
+                finish(*before)
+            make_x(group, 1, j0, width)
+            quantize("h", 1, j0, width)
+            if before is None:
+                gather_candidates(1, 1)
+            before = (j0, width)
+        quantize("x", 1, *before)
+        finish(*before)

@@ -66,6 +66,11 @@ def tile_list_foursome_invitation_scores_kernel(
         v2s_rows = load_rows("v2s_rows", 16 * R_PASSES, T, tab2_scales.rearrange("a q t -> q a t"))
         v3s_rows = load_rows("v3s_rows", 16 * R_PASSES, T, tab3_scales.rearrange("a q t -> q a t"))
 
+        warm_in = held([P, 1], F32, "warm_in")
+        warm_out = held([P, 1], F32, "warm_out")
+        nc.vector.memset(warm_in[:], 0.0)
+        nc.scalar.activation(out=warm_out[:], in_=warm_in[:], func=ACT.Silu)
+
         w4_planes = held([P, W4_PASSES * H], U8, "w4_planes")
         v_planes = held([P, V_PASSES * S], U8, "v_planes")
         c_planes = held([P, R_PASSES * 2 * S2], U8, "c_planes")

@@ -1,6 +1,7 @@
 from contextlib import ExitStack
 
 import concourse.mybir as mybir
+from concourse.masks import make_identity
 
 K, K1, T, S, H, S2 = 1536, 1024, 2048, 512, 1024, 512
 FLOPS = 2 * K * H * S + 2 * 2 * H * S2 * S
@@ -27,7 +28,9 @@ J_CHUNKS = S // JW
 M_TILES = S2 // P
 LIST_COLS = 16
 QUADS = 4
-LINE = 4
+LINE = 2
+PAIR_ROW = 96
+LONE_ROW = 80
 BANK = 512
 LAST_CHUNKS = ((0, 256), (256, 128), (384, 128))
 
@@ -40,7 +43,6 @@ def tile_list_foursome_invitation_scores_kernel(
     with ExitStack() as ctx:
         lists = ctx.enter_context(tc.tile_pool(name="lists", bufs=1))
         keep = ctx.enter_context(tc.tile_pool(name="keep", bufs=1))
-        big = ctx.enter_context(tc.tile_pool(name="big", bufs=1))
         work = ctx.enter_context(tc.tile_pool(name="work", bufs=2))
         psum_a = ctx.enter_context(tc.psum_pool(name="psum_a", bufs=4))
         psum_e = ctx.enter_context(tc.psum_pool(name="psum_e", bufs=4))
@@ -55,81 +57,84 @@ def tile_list_foursome_invitation_scores_kernel(
         nc.sync.dma_start(idx2[:], offs2)
         nc.sync.dma_start(idx3[:], offs3)
 
-        def load_rows(name, rows, width, src):
-            tile = big.tile([P, width], U8, name=name, align_bytes=64)
-            nc.scalar.dma_start(tile[P - rows : P, :].bitcast(I32), src.bitcast(I32))
-            nc.vector.memset(tile[0 : P - rows, :].bitcast(I32), 0)
-            return tile
+        def load_rows(tile, first, src):
+            rows = src.shape[0] * src.shape[1]
+            nc.scalar.dma_start(tile[first : first + rows, :].bitcast(I32), src.rearrange("a q c -> q a c").bitcast(I32))
 
-        w4s_rows = load_rows("buf_a", 16 * W4_PASSES, H, w4_scales.rearrange("a q c -> q a c"))
-        vs_rows = load_rows("buf_b", 16 * V_PASSES, T, tab_scales.rearrange("a q t -> q a t"))
-        v2s_rows = load_rows("v2s_rows", 16 * R_PASSES, T, tab2_scales.rearrange("a q t -> q a t"))
-        v3s_rows = load_rows("v3s_rows", 16 * R_PASSES, T, tab3_scales.rearrange("a q t -> q a t"))
-
+        vs_rows = held([P, T], U8, "vs_rows")
+        w4s_rows = held([P, H], U8, "w4s_rows")
+        v2s_rows = held([P, T], U8, "v2s_rows")
+        v3s_rows = held([P, T], U8, "v3s_rows")
+        load_rows(vs_rows, PAIR_ROW, tab_scales[0:W4_PASSES])
+        load_rows(vs_rows, LONE_ROW, tab_scales[W4_PASSES:V_PASSES])
+        load_rows(w4s_rows, PAIR_ROW, w4_scales)
+        load_rows(v2s_rows, PAIR_ROW, tab2_scales)
+        load_rows(v3s_rows, PAIR_ROW, tab3_scales)
         warm_in = held([P, 1], F32, "warm_in")
         warm_out = held([P, 1], F32, "warm_out")
         nc.vector.memset(warm_in[:], 0.0)
         nc.scalar.activation(out=warm_out[:], in_=warm_in[:], func=ACT.Silu)
+        nc.vector.memset(vs_rows[0:LONE_ROW, :].bitcast(I32), 0)
+        nc.vector.memset(w4s_rows[0:PAIR_ROW, :].bitcast(I32), 0)
 
-        w4_planes = held([P, W4_PASSES * H], U8, "w4_planes")
-        v_planes = held([P, V_PASSES * S], U8, "v_planes")
+        w4v_planes = held([P, W4_PASSES, H + S], U8, "w4v_planes")
         c_planes = held([P, R_PASSES * 2 * S2], U8, "c_planes")
-        for planes in (w4_planes, v_planes, c_planes):
-            nc.vector.memset(planes[:].bitcast(I32), 0)
+        nc.vector.memset(w4v_planes[:].rearrange("p a c -> p (a c)").bitcast(I32), 0)
 
-        def place_rows(queue, planes, rows, count):
+        def place_rows(queue, planes, rows, first, count):
             per_quad = count // QUADS
             for q in range(QUADS):
-                r0 = P - count + per_quad * q
-                queue.dma_start(planes[32 * q : 32 * q + 4, :].bitcast(I32), rows[r0 : r0 + per_quad, :].bitcast(I32))
+                r0 = first + per_quad * q
+                queue.dma_start(planes[32 * q : 32 * q + 4].bitcast(I32), rows[r0 : r0 + per_quad, :].bitcast(I32))
 
-        b1_sb = held([P, R_PASSES, PACK], F32, "b1_sb")
-        gp_sb = held([P, R_PASSES, PACK], F32, "gp_sb")
-        gv_sb = held([P, R_PASSES, PACK], F32, "gv_sb")
-        d_sb = held([P, M_TILES], F32, "d_sb")
-        for tile, vec in ((b1_sb, b1), (gp_sb, gp), (gv_sb, gv)):
-            nc.gpsimd.dma_start(tile[:], vec.rearrange("(b p t) -> p b t", p=P, t=PACK))
-        with nc.allow_non_contiguous_dma(reason="one value of d for each output row"):
-            nc.gpsimd.dma_start(d_sb[:], d.rearrange("(u p) -> p u", p=P))
+        vec_rows = held([P, KP + P], F32, "vec_rows")
+        ident = held([P, P], F32, "ident")
+        nc.gpsimd.memset(vec_rows[:], 0.0)
+        make_identity(nc, ident[:])
+        for tile in (v2s_rows, v3s_rows):
+            nc.gpsimd.memset(tile[0:PAIR_ROW, :].bitcast(I32), 0)
+        for n, vec in enumerate((b1, gp, gv)):
+            nc.gpsimd.dma_start(vec_rows[R_PASSES * n : R_PASSES * (n + 1), 0:KP], vec.rearrange("(b r) -> b r", r=KP))
+        nc.gpsimd.dma_start(vec_rows[0:M_TILES, KP : KP + P], d.rearrange("(u p) -> u p", p=P))
+
+        nc.gpsimd.memset(c_planes[:].bitcast(I32), 0)
 
         w1_rows = w1.rearrange("(p j) c -> p j c", j=PACK)
 
-        def load_w1(b):
-            tile = big.tile([P, PACK, KP], F32, name="buf_w", align_bytes=64)
+        def load_w1(b, buf):
+            tile = held([P, PACK, KP], F32, buf)
             nc.sync.dma_start(tile[:], w1_rows[:, :, b * KP : (b + 1) * KP])
             return tile
 
         def load_words(words, a, buf):
-            tile = big.tile([P, T], U32, name=buf, align_bytes=64)
+            tile = held([P, T], U32, buf)
             nc.sync.dma_start(tile[:].bitcast(I32), words[a].rearrange("p t i -> p (t i)").bitcast(I32))
             return tile
 
-        w1_raw = [load_w1(0)]
+        w1_raw = [load_w1(0, "buf_a")]
         w4_raw = held([P, W4_PASSES, 2 * H], U8, "w4_raw")
         nc.sync.dma_start(w4_raw[:].bitcast(I32), w4_words.rearrange("a p n -> p a n").bitcast(I32))
-        v_tab = [load_words(tab_words, 0, "buf_0")]
+        v_tab = [load_words(tab_words, 0, "buf_b"), load_words(tab_words, 1, "buf_c")]
 
-        w4s_dealt = held([P, H], U8, "w4s_dealt")
+        vs_picked = held([P, S], U8, "vs_picked")
+        staged = held([P, H + S], U8, "staged")
+        nc.vector.tensor_copy(vs_picked[:], vs_rows[:].indirect(idx[:]))
         nc.vector.tensor_copy(
-            out=w4s_dealt[:].rearrange("p (b t c i) -> p b c t i", b=R_PASSES, t=PACK, i=16),
+            out=staged[:, 0:H].rearrange("p (b t c i) -> p b c t i", b=R_PASSES, t=PACK, i=16),
             in_=w4s_rows[:].rearrange("p (b c i t) -> p b c t i", b=R_PASSES, t=PACK, i=16),
         )
-        place_rows(nc.scalar, w4_planes, w4s_dealt, 16 * W4_PASSES)
-        v_tab.append(load_words(tab_words, 1, "buf_a"))
-        vs_picked = held([P, S], U8, "vs_picked")
-        nc.vector.tensor_copy(vs_picked[:], vs_rows[:].indirect(idx[:]))
-        place_rows(nc.scalar, v_planes, vs_picked, 16 * V_PASSES)
-        v_tab.append(load_words(tab_words, 2, "buf_b"))
+        nc.vector.tensor_copy(staged[:, H : H + S].bitcast(I32), vs_picked[:].bitcast(I32))
+        place_rows(nc.scalar, w4v_planes[:].rearrange("p a c -> p (a c)"), staged, PAIR_ROW, 32)
 
-        w4_dealt = [held([P, W4_PASSES, 2 * KP], U8, f"w4_dealt{b}") for b in range(R_PASSES)]
+        w4_dealt = [held([P, W4_PASSES, 2 * KP], U8, ("buf_d", "w4_dealt1")[b]) for b in range(R_PASSES)]
         w1_bf = [held([P, PACK, P, PACK], BF16, f"w1_bf{b}") for b in range(R_PASSES)]
         w1_codes = [held([P, KP], U32, f"w1_codes{b}") for b in range(R_PASSES)]
         w1_scales = [held([P, KP], U8, f"w1_scales{b}") for b in range(R_PASSES)]
 
-        def deal_w1(b, copy):
+        def deal_w1(b, copy, m0, m1):
             copy(
-                out=w1_bf[b][:].rearrange("p t m j -> p m t j"),
-                in_=w1_raw[b][:].rearrange("p j (m t) -> p m t j", t=PACK),
+                out=w1_bf[b][:, :, m0:m1, :].rearrange("p (s t) m j -> p s m j t", t=2),
+                in_=w1_raw[b][:, :, PACK * m0 : PACK * m1].rearrange("p j (m s t) -> p s m j t", s=2, t=2),
             )
 
         def quantize_w1(b):
@@ -145,21 +150,13 @@ def tile_list_foursome_invitation_scores_kernel(
                 in_=src.rearrange("p a (c i t) -> p a c t i", t=PACK, i=8),
             )
 
-        deal_w1(0, nc.scalar.copy)
-        w1_raw.append(load_w1(1))
+        deal_w1(0, nc.scalar.copy, 0, P)
+        v_tab.append(load_words(tab_words, 2, "buf_a"))
         deal_w4(0)
         quantize_w1(0)
-
-        cs_picked = held([P, 2 * S2], U8, "cs_picked")
-        nc.vector.tensor_copy(cs_picked[:, 0:S2], v2s_rows[:].indirect(idx2[:]))
-        nc.vector.tensor_copy(cs_picked[:, S2 : 2 * S2], v3s_rows[:].indirect(idx3[:]))
-        place_rows(nc.gpsimd, c_planes, cs_picked, 16 * R_PASSES)
-        deal_w4(1)
-
-        half_b1 = held([P, R_PASSES, PACK], F32, "half_b1")
-        gv_m2 = held([P, R_PASSES, PACK], F32, "gv_m2")
-        nc.vector.tensor_scalar(out=half_b1[:], in0=b1_sb[:], scalar1=0.5, scalar2=None, op0=ALU.mult)
-        nc.vector.tensor_scalar(out=gv_m2[:], in0=gv_sb[:], scalar1=-2.0, scalar2=None, op0=ALU.mult)
+        v_last_plane = held([P, S], U8, "w1_bf0")
+        nc.vector.memset(v_last_plane[:].bitcast(I32), 0)
+        place_rows(nc.sync, v_last_plane[:], vs_picked, LONE_ROW, 16)
 
         cols = JW // LIST_COLS
         v_picked = {}
@@ -167,9 +164,30 @@ def tile_list_foursome_invitation_scores_kernel(
             for jc in range(J_CHUNKS):
                 v_picked[a, jc] = held([P, JW], U32, f"v_picked{a}_{jc}")
                 nc.vector.tensor_copy(v_picked[a, jc][:], v_tab[a][:].indirect(idx[:, jc * cols : (jc + 1) * cols]))
+        w1_raw.append(load_w1(1, "buf_b"))
+        v2_tab, v3_tab = [load_words(tab2_words, 0, "buf_c")], [load_words(tab3_words, 0, "buf_a")]
 
-        v2_tab, v3_tab = [load_words(tab2_words, 0, "buf_0")], [load_words(tab3_words, 0, "buf_a")]
-        v2_tab.append(load_words(tab2_words, 1, "buf_b"))
+        by_t = psum_e.tile([P, PACK, P], F32, name="e_bank")
+        by_u = psum_e.tile([P, P], F32, name="e_bank")
+        for t in range(PACK):
+            nc.tensor.transpose(by_t[:, t, :], vec_rows[:, t:KP:PACK], ident[:])
+        nc.tensor.transpose(by_u[:], vec_rows[:, KP : KP + P], ident[:])
+        b1_gp = held([P, 2 * R_PASSES, PACK], F32, "b1_gp")
+        half_b1 = held([P, R_PASSES, PACK], F32, "half_b1")
+        gv_m2 = held([P, R_PASSES, PACK], F32, "gv_m2")
+        d_sb = held([P, M_TILES], F32, "d_sb")
+        by_row = by_t[:].rearrange("p t r -> p r t")
+        nc.vector.tensor_copy(b1_gp[:], by_row[:, 0 : 2 * R_PASSES, :])
+        nc.vector.tensor_scalar(out=half_b1[:], in0=by_row[:, 0:R_PASSES, :], scalar1=0.5, scalar2=None, op0=ALU.mult)
+        nc.vector.tensor_scalar(out=gv_m2[:], in0=by_row[:, 2 * R_PASSES : 3 * R_PASSES, :], scalar1=-2.0, scalar2=None, op0=ALU.mult)
+        nc.vector.tensor_copy(d_sb[:], by_u[:, 0:M_TILES])
+        b1_sb, gp_sb = b1_gp[:, 0:R_PASSES, :], b1_gp[:, R_PASSES : 2 * R_PASSES, :]
+
+        cs_picked = held([P, 2 * S2], U8, "cs_picked")
+        nc.vector.tensor_copy(cs_picked[:, 0:S2], v2s_rows[:].indirect(idx2[:]))
+        nc.vector.tensor_copy(cs_picked[:, S2 : 2 * S2], v3s_rows[:].indirect(idx3[:]))
+        place_rows(nc.gpsimd, c_planes[:], cs_picked, PAIR_ROW, 32)
+        deal_w4(1)
 
         def new_banks(pool, tag, width):
             per_bank = BANK // width
@@ -182,15 +200,16 @@ def tile_list_foursome_invitation_scores_kernel(
             for t in range(PACK):
                 if a < W4_PASSES:
                     lhsT = w4_dealt[b][:, a, 2 * P * t : 2 * P * (t + 1)].bitcast(FP4X4)
-                    c0 = a * H + b * KP + P * t
-                    lhsT_scale = w4_planes[:, c0 : c0 + P]
+                    lhsT_scale = w4v_planes[:, a, b * KP + P * t : b * KP + P * (t + 1)]
+                    rhs_scale = w4v_planes[:, a, H + j0 : H + j0 + width]
                 else:
                     lhsT = w1_codes[b][:, P * t : P * (t + 1)].bitcast(FP8X4)
                     lhsT_scale = w1_scales[b][:, P * t : P * (t + 1)]
+                    rhs_scale = v_last_plane[:, j0 : j0 + width]
                 nc.tensor.matmul_mx(
                     out=banks[t // per_bank][:, t % per_bank, :], lhsT=lhsT, lhsT_scale=lhsT_scale,
                     rhs=v_picked[a, jc][:, off : off + width].bitcast(FP8X4),
-                    rhs_scale=v_planes[:, a * S + j0 : a * S + j0 + width],
+                    rhs_scale=rhs_scale,
                     start=(a == 0 and t % per_bank == 0), stop=(a == V_PASSES - 1 and t % per_bank == per_bank - 1),
                 )
 
@@ -206,7 +225,7 @@ def tile_list_foursome_invitation_scores_kernel(
 
         def make_h(group, b, j0, width):
             banks, per_bank = group
-            th = work.tile([P, PACK, width], F32, name="th")
+            th = held([P, PACK, width], F32, "buf_e" if (b, j0) == (0, 0) else f"th{b}_{j0}")
             for t in range(PACK):
                 nc.scalar.activation(out=th[:, t, :], in_=banks[t // per_bank][:, t % per_bank, :], func=ACT.Tanh, bias=b1_sb[:, b, t : t + 1])
             rounded["h", b, j0] = work.tile([P, width, PACK], BF16, name="h_bf", align_bytes=64)
@@ -276,10 +295,12 @@ def tile_list_foursome_invitation_scores_kernel(
         for a in range(V_PASSES):
             for jc in range(J_CHUNKS):
                 stage1_pass(first[jc], 0, jc * JW, JW, a)
+        v2_tab.append(load_words(tab2_words, 1, "buf_d"))
         make_h(first[0], 0, 0, JW)
-        deal_w1(1, nc.vector.tensor_copy)
-        v3_tab.append(load_words(tab3_words, 1, "buf_w"))
+        v3_tab.append(load_words(tab3_words, 1, "buf_e"))
+        deal_w1(1, nc.vector.tensor_copy, 0, P // 2)
         make_x(first[0], 0, 0, JW)
+        deal_w1(1, nc.scalar.copy, P // 2, P)
         quantize_w1(1)
         quantize("h", 0, 0, JW)
         make_h(first[1], 0, JW, JW)

from contextlib import ExitStack

import concourse.mybir as mybir
from concourse.masks import make_identity

K, K1, T, S, H, S2 = 1536, 1024, 2048, 512, 1024, 512
FLOPS = 2 * K * H * S + 2 * 2 * H * S2 * S

F32 = mybir.dt.float32
BF16 = mybir.dt.bfloat16
I32 = mybir.dt.int32
U32 = mybir.dt.uint32
U16 = mybir.dt.uint16
U8 = mybir.dt.uint8
FP8X4 = mybir.dt.float8_e4m3fn_x4
FP4X4 = mybir.dt.float4_e2m1fn_x4
ACT = mybir.ActivationFunctionType
ALU = mybir.AluOpType

P = 128
PACK = 4
KP = P * PACK
V_PASSES = K // KP
W4_PASSES = K1 // KP
R_PASSES = H // KP
JW = 256
J_CHUNKS = S // JW
M_TILES = S2 // P
LIST_COLS = 16
QUADS = 4
LINE = 2
PAIR_ROW = 96
LONE_ROW = 80
BANK = 512
LAST_CHUNKS = ((0, 256), (256, 128), (384, 128))


def tile_list_foursome_invitation_scores_kernel(
    tc, tab_words, tab_scales, offs, w4_words, w4_scales, w1, b1, gp, gv,
    tab2_words, tab2_scales, offs2, tab3_words, tab3_scales, offs3, d, out,
):
    nc = tc.nc
    with ExitStack() as ctx:
        lists = ctx.enter_context(tc.tile_pool(name="lists", bufs=1))
        keep = ctx.enter_context(tc.tile_pool(name="keep", bufs=1))
        work = ctx.enter_context(tc.tile_pool(name="work", bufs=2))
        psum_a = ctx.enter_context(tc.psum_pool(name="psum_a", bufs=4))
        psum_e = ctx.enter_context(tc.psum_pool(name="psum_e", bufs=4))

        def held(shape, dtype, name):
            return keep.tile(shape, dtype, name=name, align_bytes=64)

        idx = lists.tile([P, S // LIST_COLS], U16, name="idx")
        idx2 = lists.tile([P, S2 // LIST_COLS], U16, name="idx2")
        idx3 = lists.tile([P, S2 // LIST_COLS], U16, name="idx3")
        nc.sync.dma_start(idx[:], offs)
        nc.sync.dma_start(idx2[:], offs2)
        nc.sync.dma_start(idx3[:], offs3)

        def load_rows(tile, first, src):
            rows = src.shape[0] * src.shape[1]
            nc.scalar.dma_start(tile[first : first + rows, :].bitcast(I32), src.rearrange("a q c -> q a c").bitcast(I32))

        vs_rows = held([P, T], U8, "vs_rows")
        w4s_rows = held([P, H], U8, "w4s_rows")
        v2s_rows = held([P, T], U8, "v2s_rows")
        v3s_rows = held([P, T], U8, "v3s_rows")
        load_rows(vs_rows, PAIR_ROW, tab_scales[0:W4_PASSES])
        load_rows(vs_rows, LONE_ROW, tab_scales[W4_PASSES:V_PASSES])
        load_rows(w4s_rows, PAIR_ROW, w4_scales)
        load_rows(v2s_rows, PAIR_ROW, tab2_scales)
        load_rows(v3s_rows, PAIR_ROW, tab3_scales)
        warm_in = held([P, 1], F32, "warm_in")
        warm_out = held([P, 1], F32, "warm_out")
        nc.vector.memset(warm_in[:], 0.0)
        nc.scalar.activation(out=warm_out[:], in_=warm_in[:], func=ACT.Silu)
        nc.vector.memset(vs_rows[0:LONE_ROW, :].bitcast(I32), 0)
        nc.vector.memset(w4s_rows[0:PAIR_ROW, :].bitcast(I32), 0)

        w4v_planes = held([P, W4_PASSES, H + S], U8, "w4v_planes")
        c_planes = held([P, R_PASSES * 2 * S2], U8, "c_planes")
        nc.vector.memset(w4v_planes[:].rearrange("p a c -> p (a c)").bitcast(I32), 0)

        def place_rows(queue, planes, rows, first, count):
            per_quad = count // QUADS
            for q in range(QUADS):
                r0 = first + per_quad * q
                queue.dma_start(planes[32 * q : 32 * q + 4].bitcast(I32), rows[r0 : r0 + per_quad, :].bitcast(I32))

        vec_rows = held([P, KP + P], F32, "vec_rows")
        ident = held([P, P], F32, "ident")
        nc.gpsimd.memset(vec_rows[:], 0.0)
        make_identity(nc, ident[:])
        for tile in (v2s_rows, v3s_rows):
            nc.gpsimd.memset(tile[0:PAIR_ROW, :].bitcast(I32), 0)
        for n, vec in enumerate((b1, gp, gv)):
            nc.gpsimd.dma_start(vec_rows[R_PASSES * n : R_PASSES * (n + 1), 0:KP], vec.rearrange("(b r) -> b r", r=KP))
        nc.gpsimd.dma_start(vec_rows[0:M_TILES, KP : KP + P], d.rearrange("(u p) -> u p", p=P))

        nc.gpsimd.memset(c_planes[:].bitcast(I32), 0)

        w1_rows = w1.rearrange("(p j) c -> p j c", j=PACK)

        def load_w1(b, buf):
            tile = held([P, PACK, KP], F32, buf)
            nc.sync.dma_start(tile[:], w1_rows[:, :, b * KP : (b + 1) * KP])
            return tile

        def load_words(words, a, buf):
            tile = held([P, T], U32, buf)
            nc.sync.dma_start(tile[:].bitcast(I32), words[a].rearrange("p t i -> p (t i)").bitcast(I32))
            return tile

        w1_raw = [load_w1(0, "buf_a")]
        w4_raw = held([P, W4_PASSES, 2 * H], U8, "w4_raw")
        nc.sync.dma_start(w4_raw[:].bitcast(I32), w4_words.rearrange("a p n -> p a n").bitcast(I32))
        v_tab = [load_words(tab_words, 0, "buf_b"), load_words(tab_words, 1, "buf_c")]

        vs_picked = held([P, S], U8, "vs_picked")
        staged = held([P, H + S], U8, "staged")
        nc.vector.tensor_copy(vs_picked[:], vs_rows[:].indirect(idx[:]))
        nc.vector.tensor_copy(
            out=staged[:, 0:H].rearrange("p (b t c i) -> p b c t i", b=R_PASSES, t=PACK, i=16),
            in_=w4s_rows[:].rearrange("p (b c i t) -> p b c t i", b=R_PASSES, t=PACK, i=16),
        )
        nc.vector.tensor_copy(staged[:, H : H + S].bitcast(I32), vs_picked[:].bitcast(I32))
        place_rows(nc.scalar, w4v_planes[:].rearrange("p a c -> p (a c)"), staged, PAIR_ROW, 32)

        w4_dealt = [held([P, W4_PASSES, 2 * KP], U8, ("buf_d", "w4_dealt1")[b]) for b in range(R_PASSES)]
        w1_bf = [held([P, PACK, P, PACK], BF16, f"w1_bf{b}") for b in range(R_PASSES)]
        w1_codes = [held([P, KP], U32, f"w1_codes{b}") for b in range(R_PASSES)]
        w1_scales = [held([P, KP], U8, f"w1_scales{b}") for b in range(R_PASSES)]

        def deal_w1(b, copy, m0, m1):
            copy(
                out=w1_bf[b][:, :, m0:m1, :].rearrange("p (s t) m j -> p s m j t", t=2),
                in_=w1_raw[b][:, :, PACK * m0 : PACK * m1].rearrange("p j (m s t) -> p s m j t", s=2, t=2),
            )

        def quantize_w1(b):
            nc.vector.quantize_mx(
                out=w1_codes[b][:].bitcast(FP8X4), scales=w1_scales[b][:],
                in_=w1_bf[b][:].rearrange("p t m j -> p (t m j)"),
            )

        def deal_w4(b):
            src = w4_raw[:].bitcast(U16)[:, :, b * KP : (b + 1) * KP]
            nc.scalar.copy(
                out=w4_dealt[b][:].bitcast(U16).rearrange("p a (t c i) -> p a c t i", t=PACK, i=8),
                in_=src.rearrange("p a (c i t) -> p a c t i", t=PACK, i=8),
            )

        deal_w1(0, nc.scalar.copy, 0, P)
        v_tab.append(load_words(tab_words, 2, "buf_a"))
        deal_w4(0)
        quantize_w1(0)
        v_last_plane = held([P, S], U8, "w1_bf0")
        nc.vector.memset(v_last_plane[:].bitcast(I32), 0)
        place_rows(nc.sync, v_last_plane[:], vs_picked, LONE_ROW, 16)

        cols = JW // LIST_COLS
        v_picked = {}
        for a in range(V_PASSES):
            for jc in range(J_CHUNKS):
                v_picked[a, jc] = held([P, JW], U32, f"v_picked{a}_{jc}")
                nc.vector.tensor_copy(v_picked[a, jc][:], v_tab[a][:].indirect(idx[:, jc * cols : (jc + 1) * cols]))
        w1_raw.append(load_w1(1, "buf_b"))
        v2_tab, v3_tab = [load_words(tab2_words, 0, "buf_c")], [load_words(tab3_words, 0, "buf_a")]

        by_t = psum_e.tile([P, PACK, P], F32, name="e_bank")
        by_u = psum_e.tile([P, P], F32, name="e_bank")
        for t in range(PACK):
            nc.tensor.transpose(by_t[:, t, :], vec_rows[:, t:KP:PACK], ident[:])
        nc.tensor.transpose(by_u[:], vec_rows[:, KP : KP + P], ident[:])
        b1_gp = held([P, 2 * R_PASSES, PACK], F32, "b1_gp")
        half_b1 = held([P, R_PASSES, PACK], F32, "half_b1")
        gv_m2 = held([P, R_PASSES, PACK], F32, "gv_m2")
        d_sb = held([P, M_TILES], F32, "d_sb")
        by_row = by_t[:].rearrange("p t r -> p r t")
        nc.vector.tensor_copy(b1_gp[:], by_row[:, 0 : 2 * R_PASSES, :])
        nc.vector.tensor_scalar(out=half_b1[:], in0=by_row[:, 0:R_PASSES, :], scalar1=0.5, scalar2=None, op0=ALU.mult)
        nc.vector.tensor_scalar(out=gv_m2[:], in0=by_row[:, 2 * R_PASSES : 3 * R_PASSES, :], scalar1=-2.0, scalar2=None, op0=ALU.mult)
        nc.vector.tensor_copy(d_sb[:], by_u[:, 0:M_TILES])
        b1_sb, gp_sb = b1_gp[:, 0:R_PASSES, :], b1_gp[:, R_PASSES : 2 * R_PASSES, :]

        cs_picked = held([P, 2 * S2], U8, "cs_picked")
        nc.vector.tensor_copy(cs_picked[:, 0:S2], v2s_rows[:].indirect(idx2[:]))
        nc.vector.tensor_copy(cs_picked[:, S2 : 2 * S2], v3s_rows[:].indirect(idx3[:]))
        place_rows(nc.gpsimd, c_planes[:], cs_picked, PAIR_ROW, 32)
        deal_w4(1)

        def new_banks(pool, tag, width):
            per_bank = BANK // width
            banks = [pool.tile([P, per_bank, width], F32, name=tag) for slot in range(PACK // per_bank)]
            return banks, per_bank

        def stage1_pass(group, b, j0, width, a):
            banks, per_bank = group
            jc, off = divmod(j0, JW)
            for t in range(PACK):
                if a < W4_PASSES:
                    lhsT = w4_dealt[b][:, a, 2 * P * t : 2 * P * (t + 1)].bitcast(FP4X4)
                    lhsT_scale = w4v_planes[:, a, b * KP + P * t : b * KP + P * (t + 1)]
                    rhs_scale = w4v_planes[:, a, H + j0 : H + j0 + width]
                else:
                    lhsT = w1_codes[b][:, P * t : P * (t + 1)].bitcast(FP8X4)
                    lhsT_scale = w1_scales[b][:, P * t : P * (t + 1)]
                    rhs_scale = v_last_plane[:, j0 : j0 + width]
                nc.tensor.matmul_mx(
                    out=banks[t // per_bank][:, t % per_bank, :], lhsT=lhsT, lhsT_scale=lhsT_scale,
                    rhs=v_picked[a, jc][:, off : off + width].bitcast(FP8X4),
                    rhs_scale=rhs_scale,
                    start=(a == 0 and t % per_bank == 0), stop=(a == V_PASSES - 1 and t % per_bank == per_bank - 1),
                )

        rounded, codes, scales = {}, {}, {}

        def quantize(kind, b, j0, width):
            codes[kind, b, j0] = held([P, width], U32, f"{kind}_codes{b}_{j0}")
            scales[kind, b, j0] = held([P, width], U8, f"{kind}_scales{b}_{j0}")
            nc.vector.quantize_mx(
                out=codes[kind, b, j0][:].bitcast(FP8X4), scales=scales[kind, b, j0][:],
                in_=rounded[kind, b, j0][:].rearrange("p j t -> p (j t)"),
            )

        def make_h(group, b, j0, width):
            banks, per_bank = group
            th = held([P, PACK, width], F32, "buf_e" if (b, j0) == (0, 0) else f"th{b}_{j0}")
            for t in range(PACK):
                nc.scalar.activation(out=th[:, t, :], in_=banks[t // per_bank][:, t % per_bank, :], func=ACT.Tanh, bias=b1_sb[:, b, t : t + 1])
            rounded["h", b, j0] = work.tile([P, width, PACK], BF16, name="h_bf", align_bytes=64)
            nc.vector.tensor_tensor(
                out=rounded["h", b, j0][:].rearrange("p (c i) t -> p c t i", i=LINE),
                in0=th[:].rearrange("p t (c i) -> p c t i", i=LINE),
                in1=gp_sb[:, b, :].unsqueeze(1).unsqueeze(3).to_broadcast([P, width // LINE, PACK, LINE]),
                op=ALU.mult,
            )

        def make_x(group, b, j0, width):
            banks, per_bank = group
            sn = work.tile([P, PACK, width], F32, name="sn")
            sq = work.tile([P, width, PACK], F32, name="sq")
            for t in range(PACK):
                nc.scalar.activation(out=sn[:, t, :], in_=banks[t // per_bank][:, t % per_bank, :], func=ACT.Sin, bias=half_b1[:, b, t : t + 1], scale=0.5)
            nc.scalar.activation(
                out=sq[:].rearrange("p (c i) t -> p c t i", i=LINE),
                in_=sn[:].rearrange("p t (c i) -> p c t i", i=LINE), func=ACT.Square,
            )
            rounded["x", b, j0] = work.tile([P, width, PACK], BF16, name="x_bf", align_bytes=64)
            nc.vector.scalar_tensor_tensor(
                out=rounded["x", b, j0][:], in0=sq[:], scalar=-0.5,
                in1=gv_m2[:, b, :].unsqueeze(1).to_broadcast([P, width, PACK]), op0=ALU.add, op1=ALU.mult,
            )

        c_picked = {}

        def gather_candidates(n, b):
            tabs, lst = ((v2_tab, idx2), (v3_tab, idx3))[n]
            c_picked[n, b] = held([P, S2], U32, f"c_picked{n}_{b}")
            nc.vector.tensor_copy(c_picked[n, b][:], tabs[b][:].indirect(lst[:]))

        def stage2_pass(group, n, kind, b, j0, width):
            banks, per_bank = group
            first = j0 if b == R_PASSES - 1 else j0 // JW * JW
            off = j0 - first
            for u in range(M_TILES):
                c0 = (2 * b + n) * S2 + P * u
                nc.tensor.matmul_mx(
                    out=banks[u // per_bank][:, u % per_bank, :],
                    lhsT=c_picked[n, b][:, P * u : P * (u + 1)].bitcast(FP8X4), lhsT_scale=c_planes[:, c0 : c0 + P],
                    rhs=codes[kind, b, first][:, off : off + width].bitcast(FP8X4),
                    rhs_scale=scales[kind, b, first][:, off : off + width],
                    start=(b == 0 and u % per_bank == 0), stop=(b == R_PASSES - 1 and u % per_bank == per_bank - 1),
                )

        out_rows = out.rearrange("(u p) j -> p u j", p=P)

        def finish(j0, width):
            e2 = new_banks(psum_e, "e_bank", width)
            e3 = new_banks(psum_e, "e_bank", width)
            per_bank = e2[1]
            for b in range(R_PASSES):
                stage2_pass(e2, 0, "h", b, j0, width)
                stage2_pass(e3, 1, "x", b, j0, width)
            de2 = work.tile([P, M_TILES, width], F32, name="de2")
            res = work.tile([P, M_TILES, width], F32, name="res")
            for u in range(M_TILES):
                nc.scalar.activation(out=de2[:, u, :], in_=e2[0][u // per_bank][:, u % per_bank, :], func=ACT.Copy, scale=d_sb[:, u : u + 1])
            for g, bank in enumerate(e3[0]):
                tiles = slice(per_bank * g, per_bank * (g + 1))
                nc.vector.tensor_tensor(out=res[:, tiles, :], in0=bank[:], in1=de2[:, tiles, :], op=ALU.add)
                nc.sync.dma_start(out_rows[:, tiles, j0 : j0 + width], res[:, tiles, :])

        first = [new_banks(psum_a, "a_bank", JW) for chunk in range(J_CHUNKS)]
        for a in range(V_PASSES):
            for jc in range(J_CHUNKS):
                stage1_pass(first[jc], 0, jc * JW, JW, a)
        v2_tab.append(load_words(tab2_words, 1, "buf_d"))
        make_h(first[0], 0, 0, JW)
        v3_tab.append(load_words(tab3_words, 1, "buf_e"))
        deal_w1(1, nc.vector.tensor_copy, 0, P // 2)
        make_x(first[0], 0, 0, JW)
        deal_w1(1, nc.scalar.copy, P // 2, P)
        quantize_w1(1)
        quantize("h", 0, 0, JW)
        make_h(first[1], 0, JW, JW)
        quantize("x", 0, 0, JW)
        gather_candidates(0, 0)
        make_x(first[1], 0, JW, JW)
        quantize("h", 0, JW, JW)
        gather_candidates(1, 0)
        quantize("x", 0, JW, JW)
        before = None
        for j0, width in LAST_CHUNKS:
            group = new_banks(psum_a, "a_bank", width)
            for a in range(V_PASSES):
                stage1_pass(group, 1, j0, width, a)
            make_h(group, 1, j0, width)
            if before is None:
                gather_candidates(0, 1)
            else:
                quantize("x", 1, *before)
                finish(*before)
            make_x(group, 1, j0, width)
            quantize("h", 1, j0, width)
            if before is None:
                gather_candidates(1, 1)
            before = (j0, width)
        quantize("x", 1, *before)
        finish(*before)
